import numpy as np
import ml_dtypes


def mxq(x, axis, fmt="e4m3"):
    dtype, down = {"e4m3": (ml_dtypes.float8_e4m3fn, 7), "e5m2": (ml_dtypes.float8_e5m2, 14)}[fmt]
    v = np.moveaxis(np.asarray(x, np.float32).astype(ml_dtypes.bfloat16).astype(np.float64), axis, -1)
    blocks = v.reshape(v.shape[:-1] + (-1, 32))
    amax = np.abs(blocks).max(-1, keepdims=True)
    byte = np.maximum(np.where(amax > 0, np.frexp(amax)[1] - 1 + 127, 0) - down, 1)
    scale = np.exp2(byte - 127.0)
    codes = (blocks / scale).astype(np.float32).astype(dtype).astype(np.float64)
    return np.moveaxis((codes * scale).reshape(v.shape), -1, axis)


WIDE = False


def mx_kscale(k):
    if not WIDE:
        return np.ones(k)
    levels = np.array([30, -30])
    if k % 512:
        return np.exp2(np.random.permutation(np.resize(levels, k // 32))).repeat(32)
    a = np.empty((k // 512, 16))
    for p in range(k // 512):
        a[p, :8] = np.random.permutation(np.resize(levels, 8))
        for g in range(8):
            far = levels[np.abs(levels - a[p, g]) >= 10]
            a[p, g + 8] = far[np.random.randint(len(far))]
    return np.exp2(a.ravel()).repeat(32)


def f64(x):
    return np.asarray(x).astype(np.float64)


E2M1 = np.array([0.0, 0.5, 1.0, 1.5, 2.0, 3.0, 4.0, 6.0, -0.0, -0.5, -1.0, -1.5, -2.0, -3.0, -4.0, -6.0])


def pack_weight(w, fmt):
    k, n = w.shape
    w = f64(np.asarray(w, np.float32).astype(ml_dtypes.bfloat16)).reshape(k // 32, 32, n)
    amax = np.abs(w).max(1)
    if fmt == "e4m3":
        byte = np.frexp(amax)[1] - 1 + 127 - 7
    else:
        mant, ex = np.frexp(amax / 6.0)
        byte = np.where(mant > 0.5, ex, ex - 1) + 127
    byte = np.clip(np.where(amax > 0, byte, 1), 1, 254)
    scaled = (w * np.exp2(127.0 - byte)[:, None, :]).reshape(k, n).astype(np.float32)
    by_word = np.ascontiguousarray(scaled.reshape(k // 512, 128, 4, n).transpose(0, 1, 3, 2))
    if fmt == "e4m3":
        words = by_word.astype(ml_dtypes.float8_e4m3fn).view(np.uint8)
    else:
        c = by_word.astype(ml_dtypes.float4_e2m1fn).view(np.uint8) & 0xF
        words = (c[..., 0::2] | (c[..., 1::2] << 4)).reshape(k // 512, 128, 2 * n)
    return np.ascontiguousarray(words), np.ascontiguousarray(byte.astype(np.uint8).reshape(k // 512, 16, n))


def unpack_weight(words, scales, fmt):
    g, _, n = scales.shape
    words = np.ascontiguousarray(words).reshape(g, 128, n, -1)
    if fmt == "e4m3":
        vals = words.view(ml_dtypes.float8_e4m3fn).astype(np.float64)
    else:
        nib = np.empty((g, 128, n, 4), np.uint8)
        nib[..., 0::2] = words & 0xF
        nib[..., 1::2] = words >> 4
        vals = E2M1[nib]
    vals = vals * np.repeat(np.exp2(scales.astype(np.float64) - 127.0), 8, axis=1)[..., None]
    return vals.transpose(0, 1, 3, 2).reshape(g * 512, n)


def planes(y):
    n, m = y.shape
    v = y.astype(np.float32).astype(ml_dtypes.bfloat16).astype(np.float64).reshape(n // 32, 32, m)
    top = np.abs(v).max(1)
    byte = np.clip(np.where(top > 0, np.frexp(top)[1] - 1 + 127 - 7, 1), 1, 254)
    codes = (v * np.exp2(127.0 - byte)[:, None, :]).reshape(n, m).astype(np.float32).astype(ml_dtypes.float8_e4m3fn).view(np.uint8)
    words = codes.reshape(n // 512, 128, 4, m).transpose(0, 1, 3, 2)
    return np.ascontiguousarray(words), np.ascontiguousarray(byte.astype(np.uint8).reshape(n // 512, 16, m))


K, L, R, M, T = 1536, 1536, 512, 1536, 512


def setup_inputs():
    n = np.random.standard_normal
    s1 = mx_kscale(K)[:, None]
    s2 = mx_kscale(L)[:, None]
    u = mx_kscale(R)[:, None]
    p_w = pack_weight(n((R, M)) / np.sqrt(R) / u, "e2m1")
    return {
        "x": (n((K, T)) * s1).astype(np.float32),
        "wx": (n((K, R)) / np.sqrt(K) / s1 * u.T).astype(np.float32),
        "c": (n((L, T)) * s2).astype(np.float32),
        "wc": (n((L, R)) / np.sqrt(L) / s2).astype(np.float32),
        "w_words": p_w[0],
        "w_scales": p_w[1],
    }


def reference(x, wx, c, wc, w_words, w_scales):
    x_ = mxq(f64(x), 0, "e4m3")
    wx_ = mxq(f64(wx), 0, "e4m3")
    c_ = mxq(f64(c), 0, "e5m2")
    wc_ = mxq(f64(wc), 0, "e4m3")
    w_ = unpack_weight(w_words, w_scales, "e2m1")
    h_ = mxq((wx_.T @ x_) * (wc_.T @ c_), 0, "e4m3")
    y = h_.T @ w_
    out_0 = np.maximum(y, 0.0) ** 2
    return (out_0,) + planes(out_0)

@@ -1,0 +1,273 @@
+from contextlib import ExitStack
+
+import concourse.mybir as mybir
+
+K, R, M, T = 1536, 512, 1536, 512
+FLOPS = 2 * K * R * T * 2 + 2 * R * M * T
+
+F32 = mybir.dt.float32
+BF16 = mybir.dt.bfloat16
+U32 = mybir.dt.uint32
+I32 = mybir.dt.int32
+U8 = mybir.dt.uint8
+E4M3 = mybir.dt.float8_e4m3fn_x4
+E5M2 = mybir.dt.float8_e5m2_x4
+E2M1 = mybir.dt.float4_e2m1fn_x4
+ACT = mybir.ActivationFunctionType
+ALU = mybir.AluOpType
+
+P = 128
+PACK = 4
+K_PASS = P * PACK
+PASSES = K // K_PASS
+BANK = 512
+QUARTER = T // 4
+HALF = T // 2
+X_PIECES = [(0, 0, 256), (1, 0, 256), (2, 0, 256), (0, 256, 256), (1, 256, 256), (2, 256, 128), (2, 384, 128)]
+CHUNKS = [(0, 512), (512, 512), (1024, 256), (1280, 128), (1408, 128)]
+
+
+def tile_mix_bilin_tm_pl_relu2_kernel(tc, x, wx, c, wc, w_words, w_scales, out_0, out_1, out_2):
+    nc = tc.nc
+    with ExitStack() as ctx:
+        keep = ctx.enter_context(tc.tile_pool(name="keep", bufs=1))
+        stage = ctx.enter_context(tc.tile_pool(name="stage", bufs=4))
+        psum = ctx.enter_context(tc.psum_pool(name="psum", bufs=1))
+        ctx.enter_context(tc.manual_schedule())
+
+        def load(src, name, a, t0, width):
+            raw = keep.tile([P, PACK, width], F32, name="raw_%s%d_%d" % (name, a, t0))
+            rows = src[a * K_PASS : (a + 1) * K_PASS, t0 : t0 + width]
+            nc.sync.dma_start(out=raw[:], in_=rows.rearrange("(p j) w -> p j w", j=PACK))
+            return raw
+
+        def copy_on(engine, out, in_):
+            if engine == "S":
+                nc.scalar.copy(out=out, in_=in_)
+            else:
+                nc.vector.tensor_copy(out=out, in_=in_)
+
+        def round_plain(engine, raw):
+            width = raw.shape[2]
+            grouped = stage.tile([P, 2048], BF16, name="grouped", align_bytes=64)
+            view = grouped[:, 0 : PACK * width]
+            copy_on(engine, view.rearrange("p (c i j) -> p c j i", i=4, j=PACK), raw[:].rearrange("p j (c i) -> p c j i", i=4))
+            return view
+
+        def round_dealt(engine, raw):
+            grouped = stage.tile([P, 2048], BF16, name="grouped", align_bytes=64)
+            copy_on(engine, grouped[:].rearrange("p (s m j) -> p m s j", s=PACK, j=PACK), raw[:].rearrange("p j (m s) -> p m s j", s=PACK))
+            return grouped[:]
+
+        def quantize(view, name, fmt):
+            width = view.shape[1] // PACK
+            codes = keep.tile([P, width], U32, name="codes_" + name, align_bytes=64)
+            scales = keep.tile([P, width], U8, name="scales_" + name, align_bytes=64)
+            nc.vector.quantize_mx(out=codes[:].bitcast(fmt), scales=scales[:], in_=view)
+            return codes, scales
+
+        def bank(b):
+            return psum.tile([P, BANK], F32, name="bank%d" % b)
+
+        warm = keep.tile([P, 8], F32, name="warm")
+        warm2 = keep.tile([P, 8], F32, name="warm2")
+        w_sc = keep.tile([P, M], U8, name="w_sc", align_bytes=64)
+        w_cd = keep.tile([P, 2 * M], U8, name="w_cd", align_bytes=64)
+        nc.vector.memset(w_sc[:].bitcast(I32), 0)
+        nc.vector.memset(warm[:], 1.0)
+        nc.scalar.activation(out=warm2[:], in_=warm[:], func=ACT.Square)
+
+        raw_wc, raw_c, raw_wx, raw_x = {}, {}, {}, []
+        raw_wc[0] = load(wc, "wc", 0, 0, R)
+        for q in range(4):
+            nc.sync.dma_start(out=w_sc[32 * q : 32 * q + 4, :].bitcast(I32), in_=w_scales[0, 4 * q : 4 * q + 4, :].bitcast(I32))
+        for a in range(PASSES):
+            if a + 1 < PASSES:
+                raw_wc[a + 1] = load(wc, "wc", a + 1, 0, R)
+            raw_c[a] = load(c, "c", a, 0, T)
+        for a in range(PASSES):
+            raw_wx[a] = load(wx, "wx", a, 0, R)
+        for a, t0, width in X_PIECES:
+            raw_x.append(load(x, "x", a, t0, width))
+        nc.sync.dma_start(out=w_cd[:].bitcast(I32), in_=w_words[0].bitcast(I32))
+
+        pc_banks = [bank(j) for j in range(PACK)]
+        wc_q = [quantize(round_dealt("S", raw_wc[0]), "wc0", E4M3)]
+        for a in range(PASSES):
+            if a + 1 < PASSES:
+                g_w = round_dealt("S", raw_wc[a + 1])
+            g_c = round_plain("V", raw_c[a])
+            if a + 1 < PASSES:
+                wc_q.append(quantize(g_w, "wc%d" % (a + 1), E4M3))
+            cq, cs = quantize(g_c, "c%d" % a, E5M2)
+            wq, ws = wc_q[a]
+            for j in range(PACK):
+                cols = slice(P * j, P * (j + 1))
+                nc.tensor.matmul_mx(out=pc_banks[j][:], lhsT=wq[:, cols].bitcast(E4M3), lhsT_scale=ws[:, cols],
+                                    rhs=cq[:].bitcast(E5M2), rhs_scale=cs[:], start=(a == 0), stop=(a == PASSES - 1))
+
+        pc_rows = keep.tile([P, PACK, T], F32, name="pc_rows")
+
+        def pc_out(j, engine):
+            copy_on(engine, pc_rows[:, j, :].rearrange("p (q i m) -> p q i m", q=4, i=PACK),
+                    pc_banks[j][:].rearrange("p (q m i) -> p q i m", q=4, i=PACK))
+
+        g_wx0 = round_dealt("V", raw_wx[0])
+        for j in range(PACK):
+            pc_out(j, "S")
+        wx_q = [quantize(g_wx0, "wx0", E4M3)]
+        g_wx1 = round_dealt("S", raw_wx[1])
+        pc_words = keep.tile([P, T * PACK], F32, name="pc_words")
+        nc.vector.tensor_copy(out=pc_words[:].rearrange("p (c i j) -> p c j i", i=2, j=PACK),
+                              in_=pc_rows[:].rearrange("p j (c i) -> p c j i", i=2))
+        g_wx2 = round_dealt("V", raw_wx[2])
+        wx_q.append(quantize(g_wx1, "wx1", E4M3))
+        wx_q.append(quantize(g_wx2, "wx2", E4M3))
+
+        px_banks = [bank(4 + q) for q in range(4)]
+        h_bf = keep.tile([P, 2, PACK, HALF], BF16, name="h_bf", align_bytes=64)
+        h_cd = keep.tile([P, T], U32, name="h_cd", align_bytes=64)
+        h_sc = keep.tile([P, T], U8, name="h_sc", align_bytes=64)
+
+        def x_round(n, engine):
+            return round_plain(engine, raw_x[n])
+
+        def x_mul(n, view):
+            a, t0, width = X_PIECES[n]
+            xq, xs = quantize(view, "x%d" % n, E4M3)
+            wq, ws = wx_q[a]
+            for u in range(width // QUARTER):
+                q = t0 // QUARTER + u
+                tc_ = slice(QUARTER * u, QUARTER * (u + 1))
+                for j in range(PACK):
+                    cols = slice(P * j, P * (j + 1))
+                    nc.tensor.matmul_mx(out=px_banks[q][:, cols], lhsT=wq[:, cols].bitcast(E4M3), lhsT_scale=ws[:, cols],
+                                        rhs=xq[:, tc_].bitcast(E4M3), rhs_scale=xs[:, tc_],
+                                        start=(a == 0 and j == 0), stop=(a == PASSES - 1 and j == PACK - 1))
+
+        def h_product(q):
+            nc.vector.tensor_tensor(
+                out=h_bf[:, q // 2, :, P * (q % 2) : P * (q % 2 + 1)].rearrange("p i (m j) -> p i m j", j=PACK),
+                in0=px_banks[q][:].rearrange("p (j m i) -> p i m j", j=PACK, i=PACK),
+                in1=pc_words[:, BANK * q : BANK * (q + 1)].rearrange("p (i m j) -> p i m j", i=PACK, j=PACK),
+                op=ALU.mult)
+
+        def h_quantize(half, i):
+            cols = slice(P * i + 64 * half, P * i + 64 * (half + 1))
+            nc.vector.quantize_mx(out=h_cd[:, cols].bitcast(E4M3), scales=h_sc[:, cols], in_=h_bf[:, half, i, :])
+
+        v0 = x_round(0, "S")
+        v1 = x_round(1, "S")
+        x_mul(0, v0)
+        v2 = x_round(2, "V")
+        x_mul(1, v1)
+        x_mul(2, v2)
+        v3 = x_round(3, "S")
+        v4 = x_round(4, "S")
+        v5 = x_round(5, "S")
+        h_product(0)
+        x_mul(3, v3)
+        h_product(1)
+        v6 = x_round(6, "V")
+        x_mul(4, v4)
+        x_mul(6, v6)
+        x_mul(5, v5)
+        for i in range(PACK):
+            h_quantize(0, i)
+        h_product(3)
+        h_product(2)
+        for i in range(PACK):
+            h_quantize(1, i)
+
+        o_cd = keep.tile([P, M], U32, name="o_cd", align_bytes=64)
+        o_sc = keep.tile([P, M], U8, name="o_sc", align_bytes=64)
+        out_rows = out_0.rearrange("(p i) n -> p i n", i=PACK)
+        out_words = out_1[0].rearrange("p n t -> p (n t)").bitcast(I32)
+        units = []
+        for ci, (n0, width) in enumerate(CHUNKS):
+            per = BANK // width
+            for i0 in range(0, PACK, per):
+                units.append((ci, i0, per))
+        o_tiles = [keep.tile([P, PACK, width], F32, name="o%d" % ci) for ci, (n0, width) in enumerate(CHUNKS)]
+        y_banks, relus, views = {}, {}, {}
+
+        def y_mul(u):
+            ci, i0, per = units[u]
+            n0, width = CHUNKS[ci]
+            y_banks[u] = bank(u % 8)
+            for s in range(per):
+                cols = slice(P * (i0 + s), P * (i0 + s + 1))
+                nc.tensor.matmul_mx(out=y_banks[u][:, width * s : width * (s + 1)], lhsT=h_cd[:, cols].bitcast(E4M3), lhsT_scale=h_sc[:, cols],
+                                    rhs=w_cd[:, 2 * n0 : 2 * (n0 + width)].bitcast(E2M1), rhs_scale=w_sc[:, n0 : n0 + width],
+                                    start=True, stop=True)
+
+        def relu(u, engine):
+            relus[u] = stage.tile([P, BANK], F32, name="relu", bufs=8)
+            if engine == "S":
+                nc.scalar.activation(out=relus[u][:], in_=y_banks[u][:], func=ACT.Relu)
+            else:
+                nc.vector.tensor_scalar_max(out=relus[u][:], in0=y_banks[u][:], scalar1=0.0)
+            if u + 8 < len(units):
+                y_mul(u + 8)
+
+        def square(u):
+            ci, i0, per = units[u]
+            n0, width = CHUNKS[ci]
+            nc.scalar.activation(out=o_tiles[ci][:, i0 : i0 + per, :].rearrange("p i n -> p (i n)"), in_=relus[u][:], func=ACT.Square)
+            nc.sync.dma_start(out=out_rows[:, i0 : i0 + per, n0 : n0 + width], in_=o_tiles[ci][:, i0 : i0 + per, :])
+
+        def o_round(ci):
+            views[ci] = round_plain("V", o_tiles[ci])
+
+        def o_quantize(ci):
+            n0, width = CHUNKS[ci]
+            nc.vector.quantize_mx(out=o_cd[:, n0 : n0 + width].bitcast(E4M3), scales=o_sc[:, n0 : n0 + width], in_=views[ci])
+
+        def o_store(n0, n1):
+            nc.sync.dma_start(out=out_words[:, n0:n1], in_=o_cd[:, n0:n1].bitcast(I32))
+
+        def scale_store(queue, n0, n1):
+            for q in range(4):
+                queue.dma_start(out=out_2[0, 4 * q : 4 * q + 4, n0:n1].bitcast(I32), in_=o_sc[32 * q : 32 * q + 4, n0:n1].bitcast(I32))
+
+        for u in range(8):
+            y_mul(u)
+        relu(0, "S")
+        relu(1, "V")
+        relu(2, "S")
+        relu(3, "V")
+        square(0)
+        relu(4, "V")
+        square(1)
+        relu(5, "V")
+        square(2)
+        relu(6, "V")
+        square(3)
+        relu(7, "V")
+        square(4)
+        o_round(0)
+        square(5)
+        relu(8, "V")
+        square(6)
+        o_quantize(0)
+        square(7)
+        o_store(0, 512)
+        o_round(1)
+        relu(9, "S")
+        square(8)
+        relu(10, "S")
+        square(9)
+        o_quantize(1)
+        o_round(2)
+        o_store(512, 1024)
+        relu(11, "S")
+        square(10)
+        square(11)
+        o_quantize(2)
+        o_round(3)
+        o_round(4)
+        o_quantize(3)
+        o_quantize(4)
+        o_store(1024, 1280)
+        o_store(1280, 1536)
+        scale_store(nc.scalar, 0, M)

@@ -24,14 +24,14 @@ BANK = 512
 QUARTER = T // 4
 HALF = T // 2
 X_PIECES = [(0, 0, 256), (1, 0, 256), (2, 0, 256), (0, 256, 256), (1, 256, 256), (2, 256, 128), (2, 384, 128)]
-CHUNKS = [(0, 512), (512, 512), (1024, 256), (1280, 128), (1408, 128)]
+CHUNKS = [(0, 512), (512, 512), (1024, 256), (1280, 256)]
 
 
 def tile_mix_bilin_tm_pl_relu2_kernel(tc, x, wx, c, wc, w_words, w_scales, out_0, out_1, out_2):
     nc = tc.nc
     with ExitStack() as ctx:
         keep = ctx.enter_context(tc.tile_pool(name="keep", bufs=1))
-        stage = ctx.enter_context(tc.tile_pool(name="stage", bufs=4))
+        stage = ctx.enter_context(tc.tile_pool(name="stage", bufs=5))
         psum = ctx.enter_context(tc.psum_pool(name="psum", bufs=1))
         ctx.enter_context(tc.manual_schedule())
 
@@ -51,7 +51,7 @@ def tile_mix_bilin_tm_pl_relu2_kernel(tc, x, wx, c, wc, w_words, w_scales, out_0
             width = raw.shape[2]
             grouped = stage.tile([P, 2048], BF16, name="grouped", align_bytes=64)
             view = grouped[:, 0 : PACK * width]
-            copy_on(engine, view.rearrange("p (c i j) -> p c j i", i=4, j=PACK), raw[:].rearrange("p j (c i) -> p c j i", i=4))
+            copy_on(engine, view.rearrange("p (c i j) -> p c j i", i=4, j=PACK), raw.rearrange("p j (c i) -> p c j i", i=4))
             return view
 
         def round_dealt(engine, raw):
@@ -79,8 +79,6 @@ def tile_mix_bilin_tm_pl_relu2_kernel(tc, x, wx, c, wc, w_words, w_scales, out_0
 
         raw_wc, raw_c, raw_wx, raw_x = {}, {}, {}, []
         raw_wc[0] = load(wc, "wc", 0, 0, R)
-        for q in range(4):
-            nc.sync.dma_start(out=w_sc[32 * q : 32 * q + 4, :].bitcast(I32), in_=w_scales[0, 4 * q : 4 * q + 4, :].bitcast(I32))
         for a in range(PASSES):
             if a + 1 < PASSES:
                 raw_wc[a + 1] = load(wc, "wc", a + 1, 0, R)
@@ -90,13 +88,15 @@ def tile_mix_bilin_tm_pl_relu2_kernel(tc, x, wx, c, wc, w_words, w_scales, out_0
         for a, t0, width in X_PIECES:
             raw_x.append(load(x, "x", a, t0, width))
         nc.sync.dma_start(out=w_cd[:].bitcast(I32), in_=w_words[0].bitcast(I32))
+        for q in range(4):
+            nc.sync.dma_start(out=w_sc[32 * q : 32 * q + 4, :].bitcast(I32), in_=w_scales[0, 4 * q : 4 * q + 4, :].bitcast(I32))
 
         pc_banks = [bank(j) for j in range(PACK)]
         wc_q = [quantize(round_dealt("S", raw_wc[0]), "wc0", E4M3)]
         for a in range(PASSES):
             if a + 1 < PASSES:
                 g_w = round_dealt("S", raw_wc[a + 1])
-            g_c = round_plain("V", raw_c[a])
+            g_c = round_plain("V", raw_c[a][:])
             if a + 1 < PASSES:
                 wc_q.append(quantize(g_w, "wc%d" % (a + 1), E4M3))
             cq, cs = quantize(g_c, "c%d" % a, E5M2)
@@ -112,72 +112,85 @@ def tile_mix_bilin_tm_pl_relu2_kernel(tc, x, wx, c, wc, w_words, w_scales, out_0
             copy_on(engine, pc_rows[:, j, :].rearrange("p (q i m) -> p q i m", q=4, i=PACK),
                     pc_banks[j][:].rearrange("p (q m i) -> p q i m", q=4, i=PACK))
 
+        pc_words = keep.tile([P, T * PACK], F32, name="pc_words")
+
+        def pc_weave(half, engine):
+            copy_on(engine, pc_words[:, PACK * HALF * half : PACK * HALF * (half + 1)].rearrange("p (c i j) -> p c j i", i=2, j=PACK),
+                    pc_rows[:, :, HALF * half : HALF * (half + 1)].rearrange("p j (c i) -> p c j i", i=2))
+
         g_wx0 = round_dealt("V", raw_wx[0])
         for j in range(PACK):
             pc_out(j, "S")
         wx_q = [quantize(g_wx0, "wx0", E4M3)]
-        g_wx1 = round_dealt("S", raw_wx[1])
-        pc_words = keep.tile([P, T * PACK], F32, name="pc_words")
-        nc.vector.tensor_copy(out=pc_words[:].rearrange("p (c i j) -> p c j i", i=2, j=PACK),
-                              in_=pc_rows[:].rearrange("p j (c i) -> p c j i", i=2))
-        g_wx2 = round_dealt("V", raw_wx[2])
+        g_wx1 = round_dealt("V", raw_wx[1])
+        pc_weave(0, "S")
+        pc_weave(1, "S")
         wx_q.append(quantize(g_wx1, "wx1", E4M3))
-        wx_q.append(quantize(g_wx2, "wx2", E4M3))
+        g_wx2 = round_dealt("V", raw_wx[2])
 
         px_banks = [bank(4 + q) for q in range(4)]
-        h_bf = keep.tile([P, 2, PACK, HALF], BF16, name="h_bf", align_bytes=64)
+        h_bf = keep.tile([P, PACK, T], BF16, name="h_bf", align_bytes=64)
         h_cd = keep.tile([P, T], U32, name="h_cd", align_bytes=64)
         h_sc = keep.tile([P, T], U8, name="h_sc", align_bytes=64)
 
-        def x_round(n, engine):
-            return round_plain(engine, raw_x[n])
+        x_views, x_q = {}, {}
 
-        def x_mul(n, view):
+        def x_round(n, q0, q1, engine):
             a, t0, width = X_PIECES[n]
-            xq, xs = quantize(view, "x%d" % n, E4M3)
+            x_views[a, q0] = round_plain(engine, raw_x[n][:, :, QUARTER * q0 - t0 : QUARTER * q1 - t0])
+
+        def x_quantize(a, q0):
+            view = x_views[a, q0]
+            xq, xs = quantize(view, "x%d_%d" % (a, q0), E4M3)
+            for u in range(view.shape[1] // BANK):
+                x_q[a, q0 + u] = (xq[:, QUARTER * u : QUARTER * (u + 1)], xs[:, QUARTER * u : QUARTER * (u + 1)])
+                px_mul(a, q0 + u)
+
+        def px_mul(a, q):
+            xq, xs = x_q[a, q]
             wq, ws = wx_q[a]
-            for u in range(width // QUARTER):
-                q = t0 // QUARTER + u
-                tc_ = slice(QUARTER * u, QUARTER * (u + 1))
-                for j in range(PACK):
-                    cols = slice(P * j, P * (j + 1))
-                    nc.tensor.matmul_mx(out=px_banks[q][:, cols], lhsT=wq[:, cols].bitcast(E4M3), lhsT_scale=ws[:, cols],
-                                        rhs=xq[:, tc_].bitcast(E4M3), rhs_scale=xs[:, tc_],
-                                        start=(a == 0 and j == 0), stop=(a == PASSES - 1 and j == PACK - 1))
+            for j in range(PACK):
+                cols = slice(P * j, P * (j + 1))
+                nc.tensor.matmul_mx(out=px_banks[q][:, cols], lhsT=wq[:, cols].bitcast(E4M3), lhsT_scale=ws[:, cols],
+                                    rhs=xq.bitcast(E4M3), rhs_scale=xs,
+                                    start=(a == 0 and j == 0), stop=(a == PASSES - 1 and j == PACK - 1))
 
         def h_product(q):
             nc.vector.tensor_tensor(
-                out=h_bf[:, q // 2, :, P * (q % 2) : P * (q % 2 + 1)].rearrange("p i (m j) -> p i m j", j=PACK),
+                out=h_bf[:, :, P * q : P * (q + 1)].rearrange("p i (m j) -> p i m j", j=PACK),
                 in0=px_banks[q][:].rearrange("p (j m i) -> p i m j", j=PACK, i=PACK),
                 in1=pc_words[:, BANK * q : BANK * (q + 1)].rearrange("p (i m j) -> p i m j", i=PACK, j=PACK),
                 op=ALU.mult)
 
-        def h_quantize(half, i):
-            cols = slice(P * i + 64 * half, P * i + 64 * (half + 1))
-            nc.vector.quantize_mx(out=h_cd[:, cols].bitcast(E4M3), scales=h_sc[:, cols], in_=h_bf[:, half, i, :])
+        def h_quantize(i):
+            cols = slice(P * i, P * (i + 1))
+            nc.vector.quantize_mx(out=h_cd[:, cols].bitcast(E4M3), scales=h_sc[:, cols], in_=h_bf[:, i, :])
 
-        v0 = x_round(0, "S")
-        v1 = x_round(1, "S")
-        x_mul(0, v0)
-        v2 = x_round(2, "V")
-        x_mul(1, v1)
-        x_mul(2, v2)
-        v3 = x_round(3, "S")
-        v4 = x_round(4, "S")
-        v5 = x_round(5, "S")
+        x_round(0, 0, 2, "V")
+        wx_q.append(quantize(g_wx2, "wx2", E4M3))
+        x_quantize(0, 0)
+        x_round(1, 0, 2, "S")
+        x_round(2, 0, 1, "V")
+        x_quantize(1, 0)
+        x_quantize(2, 0)
+        x_round(2, 1, 2, "S")
+        x_quantize(2, 1)
+        x_round(3, 2, 4, "V")
+        x_quantize(0, 2)
+        x_round(4, 2, 3, "V")
+        x_round(4, 3, 4, "S")
         h_product(0)
-        x_mul(3, v3)
+        x_quantize(1, 2)
+        x_quantize(1, 3)
+        x_round(5, 2, 3, "S")
+        x_round(6, 3, 4, "V")
+        x_quantize(2, 2)
+        x_quantize(2, 3)
         h_product(1)
-        v6 = x_round(6, "V")
-        x_mul(4, v4)
-        x_mul(6, v6)
-        x_mul(5, v5)
-        for i in range(PACK):
-            h_quantize(0, i)
-        h_product(3)
         h_product(2)
+        h_product(3)
         for i in range(PACK):
-            h_quantize(1, i)
+            h_quantize(i)
 
         o_cd = keep.tile([P, M], U32, name="o_cd", align_bytes=64)
         o_sc = keep.tile([P, M], U8, name="o_sc", align_bytes=64)
@@ -214,10 +227,13 @@ def tile_mix_bilin_tm_pl_relu2_kernel(tc, x, wx, c, wc, w_words, w_scales, out_0
             ci, i0, per = units[u]
             n0, width = CHUNKS[ci]
             nc.scalar.activation(out=o_tiles[ci][:, i0 : i0 + per, :].rearrange("p i n -> p (i n)"), in_=relus[u][:], func=ACT.Square)
-            nc.sync.dma_start(out=out_rows[:, i0 : i0 + per, n0 : n0 + width], in_=o_tiles[ci][:, i0 : i0 + per, :])
+
+        def rows_store(ci, i0, i1):
+            n0, width = CHUNKS[ci]
+            nc.sync.dma_start(out=out_rows[:, i0:i1, n0 : n0 + width], in_=o_tiles[ci][:, i0:i1, :])
 
         def o_round(ci):
-            views[ci] = round_plain("V", o_tiles[ci])
+            views[ci] = round_plain("V", o_tiles[ci][:])
 
         def o_quantize(ci):
             n0, width = CHUNKS[ci]
@@ -232,42 +248,52 @@ def tile_mix_bilin_tm_pl_relu2_kernel(tc, x, wx, c, wc, w_words, w_scales, out_0
 
         for u in range(8):
             y_mul(u)
-        relu(0, "S")
-        relu(1, "V")
-        relu(2, "S")
-        relu(3, "V")
+        relu(0, "V")
+        relu(1, "S")
+        relu(2, "V")
         square(0)
-        relu(4, "V")
+        rows_store(0, 0, 1)
+        relu(3, "V")
         square(1)
-        relu(5, "V")
+        rows_store(0, 1, 2)
+        relu(4, "V")
         square(2)
-        relu(6, "V")
+        rows_store(0, 2, 3)
+        relu(5, "V")
         square(3)
-        relu(7, "V")
+        rows_store(0, 3, 4)
+        relu(6, "V")
         square(4)
-        o_round(0)
+        rows_store(1, 0, 1)
+        relu(7, "V")
         square(5)
-        relu(8, "V")
+        rows_store(1, 1, 2)
+        o_round(0)
         square(6)
-        o_quantize(0)
+        rows_store(1, 2, 3)
         square(7)
+        rows_store(1, 3, 4)
+        relu(8, "V")
+        relu(9, "S")
+        o_quantize(0)
+        square(8)
+        rows_store(2, 0, 2)
         o_store(0, 512)
         o_round(1)
-        relu(9, "S")
-        square(8)
         relu(10, "S")
         square(9)
-        o_quantize(1)
-        o_round(2)
-        o_store(512, 1024)
+        rows_store(2, 2, 4)
         relu(11, "S")
+        o_quantize(1)
         square(10)
+        rows_store(3, 0, 2)
         square(11)
+        rows_store(3, 2, 4)
+        o_store(512, 1024)
+        o_round(2)
         o_quantize(2)
         o_round(3)
-        o_round(4)
-        o_quantize(3)
-        o_quantize(4)
         o_store(1024, 1280)
+        o_quantize(3)
         o_store(1280, 1536)
-        scale_store(nc.scalar, 0, M)
+        scale_store(nc.scalar, 0, 1536)

from contextlib import ExitStack

import concourse.mybir as mybir

K, R, M, T = 1536, 512, 1536, 512
FLOPS = 2 * K * R * T * 2 + 2 * R * M * T

F32 = mybir.dt.float32
BF16 = mybir.dt.bfloat16
U32 = mybir.dt.uint32
I32 = mybir.dt.int32
U8 = mybir.dt.uint8
E4M3 = mybir.dt.float8_e4m3fn_x4
E5M2 = mybir.dt.float8_e5m2_x4
E2M1 = mybir.dt.float4_e2m1fn_x4
ACT = mybir.ActivationFunctionType
ALU = mybir.AluOpType

P = 128
PACK = 4
K_PASS = P * PACK
PASSES = K // K_PASS
BANK = 512
QUARTER = T // 4
HALF = T // 2
X_PIECES = [(0, 0, 256), (1, 0, 256), (2, 0, 256), (0, 256, 256), (1, 256, 256), (2, 256, 128), (2, 384, 128)]
CHUNKS = [(0, 512), (512, 512), (1024, 256), (1280, 256)]


def tile_mix_bilin_tm_pl_relu2_kernel(tc, x, wx, c, wc, w_words, w_scales, out_0, out_1, out_2):
    nc = tc.nc
    with ExitStack() as ctx:
        keep = ctx.enter_context(tc.tile_pool(name="keep", bufs=1))
        stage = ctx.enter_context(tc.tile_pool(name="stage", bufs=5))
        psum = ctx.enter_context(tc.psum_pool(name="psum", bufs=1))
        ctx.enter_context(tc.manual_schedule())

        def load(src, name, a, t0, width):
            raw = keep.tile([P, PACK, width], F32, name="raw_%s%d_%d" % (name, a, t0))
            rows = src[a * K_PASS : (a + 1) * K_PASS, t0 : t0 + width]
            nc.sync.dma_start(out=raw[:], in_=rows.rearrange("(p j) w -> p j w", j=PACK))
            return raw

        def copy_on(engine, out, in_):
            if engine == "S":
                nc.scalar.copy(out=out, in_=in_)
            else:
                nc.vector.tensor_copy(out=out, in_=in_)

        def round_plain(engine, raw):
            width = raw.shape[2]
            grouped = stage.tile([P, 2048], BF16, name="grouped", align_bytes=64)
            view = grouped[:, 0 : PACK * width]
            copy_on(engine, view.rearrange("p (c i j) -> p c j i", i=4, j=PACK), raw.rearrange("p j (c i) -> p c j i", i=4))
            return view

        def round_dealt(engine, raw):
            grouped = stage.tile([P, 2048], BF16, name="grouped", align_bytes=64)
            copy_on(engine, grouped[:].rearrange("p (s m j) -> p m s j", s=PACK, j=PACK), raw[:].rearrange("p j (m s) -> p m s j", s=PACK))
            return grouped[:]

        def quantize(view, name, fmt):
            width = view.shape[1] // PACK
            codes = keep.tile([P, width], U32, name="codes_" + name, align_bytes=64)
            scales = keep.tile([P, width], U8, name="scales_" + name, align_bytes=64)
            nc.vector.quantize_mx(out=codes[:].bitcast(fmt), scales=scales[:], in_=view)
            return codes, scales

        def bank(b):
            return psum.tile([P, BANK], F32, name="bank%d" % b)

        warm = keep.tile([P, 8], F32, name="warm")
        warm2 = keep.tile([P, 8], F32, name="warm2")
        w_sc = keep.tile([P, M], U8, name="w_sc", align_bytes=64)
        w_cd = keep.tile([P, 2 * M], U8, name="w_cd", align_bytes=64)
        nc.vector.memset(w_sc[:].bitcast(I32), 0)
        nc.vector.memset(warm[:], 1.0)
        nc.scalar.activation(out=warm2[:], in_=warm[:], func=ACT.Square)

        raw_wc, raw_c, raw_wx, raw_x = {}, {}, {}, []
        raw_wc[0] = load(wc, "wc", 0, 0, R)
        for a in range(PASSES):
            if a + 1 < PASSES:
                raw_wc[a + 1] = load(wc, "wc", a + 1, 0, R)
            raw_c[a] = load(c, "c", a, 0, T)
        for a in range(PASSES):
            raw_wx[a] = load(wx, "wx", a, 0, R)
        for a, t0, width in X_PIECES:
            raw_x.append(load(x, "x", a, t0, width))
        nc.sync.dma_start(out=w_cd[:].bitcast(I32), in_=w_words[0].bitcast(I32))
        for q in range(4):
            nc.sync.dma_start(out=w_sc[32 * q : 32 * q + 4, :].bitcast(I32), in_=w_scales[0, 4 * q : 4 * q + 4, :].bitcast(I32))

        pc_banks = [bank(j) for j in range(PACK)]
        wc_q = [quantize(round_dealt("S", raw_wc[0]), "wc0", E4M3)]
        for a in range(PASSES):
            if a + 1 < PASSES:
                g_w = round_dealt("S", raw_wc[a + 1])
            g_c = round_plain("V", raw_c[a][:])
            if a + 1 < PASSES:
                wc_q.append(quantize(g_w, "wc%d" % (a + 1), E4M3))
            cq, cs = quantize(g_c, "c%d" % a, E5M2)
            wq, ws = wc_q[a]
            for j in range(PACK):
                cols = slice(P * j, P * (j + 1))
                nc.tensor.matmul_mx(out=pc_banks[j][:], lhsT=wq[:, cols].bitcast(E4M3), lhsT_scale=ws[:, cols],
                                    rhs=cq[:].bitcast(E5M2), rhs_scale=cs[:], start=(a == 0), stop=(a == PASSES - 1))

        pc_rows = keep.tile([P, PACK, T], F32, name="pc_rows")

        def pc_out(j, engine):
            copy_on(engine, pc_rows[:, j, :].rearrange("p (q i m) -> p q i m", q=4, i=PACK),
                    pc_banks[j][:].rearrange("p (q m i) -> p q i m", q=4, i=PACK))

        pc_words = keep.tile([P, T * PACK], F32, name="pc_words")

        def pc_weave(half, engine):
            copy_on(engine, pc_words[:, PACK * HALF * half : PACK * HALF * (half + 1)].rearrange("p (c i j) -> p c j i", i=2, j=PACK),
                    pc_rows[:, :, HALF * half : HALF * (half + 1)].rearrange("p j (c i) -> p c j i", i=2))

        g_wx0 = round_dealt("V", raw_wx[0])
        for j in range(PACK):
            pc_out(j, "S")
        wx_q = [quantize(g_wx0, "wx0", E4M3)]
        g_wx1 = round_dealt("V", raw_wx[1])
        pc_weave(0, "S")
        pc_weave(1, "S")
        wx_q.append(quantize(g_wx1, "wx1", E4M3))
        g_wx2 = round_dealt("V", raw_wx[2])

        px_banks = [bank(4 + q) for q in range(4)]
        h_bf = keep.tile([P, PACK, T], BF16, name="h_bf", align_bytes=64)
        h_cd = keep.tile([P, T], U32, name="h_cd", align_bytes=64)
        h_sc = keep.tile([P, T], U8, name="h_sc", align_bytes=64)

        x_views, x_q = {}, {}

        def x_round(n, q0, q1, engine):
            a, t0, width = X_PIECES[n]
            x_views[a, q0] = round_plain(engine, raw_x[n][:, :, QUARTER * q0 - t0 : QUARTER * q1 - t0])

        def x_quantize(a, q0):
            view = x_views[a, q0]
            xq, xs = quantize(view, "x%d_%d" % (a, q0), E4M3)
            for u in range(view.shape[1] // BANK):
                x_q[a, q0 + u] = (xq[:, QUARTER * u : QUARTER * (u + 1)], xs[:, QUARTER * u : QUARTER * (u + 1)])
                px_mul(a, q0 + u)

        def px_mul(a, q):
            xq, xs = x_q[a, q]
            wq, ws = wx_q[a]
            for j in range(PACK):
                cols = slice(P * j, P * (j + 1))
                nc.tensor.matmul_mx(out=px_banks[q][:, cols], lhsT=wq[:, cols].bitcast(E4M3), lhsT_scale=ws[:, cols],
                                    rhs=xq.bitcast(E4M3), rhs_scale=xs,
                                    start=(a == 0 and j == 0), stop=(a == PASSES - 1 and j == PACK - 1))

        def h_product(q):
            nc.vector.tensor_tensor(
                out=h_bf[:, :, P * q : P * (q + 1)].rearrange("p i (m j) -> p i m j", j=PACK),
                in0=px_banks[q][:].rearrange("p (j m i) -> p i m j", j=PACK, i=PACK),
                in1=pc_words[:, BANK * q : BANK * (q + 1)].rearrange("p (i m j) -> p i m j", i=PACK, j=PACK),
                op=ALU.mult)

        def h_quantize(i):
            cols = slice(P * i, P * (i + 1))
            nc.vector.quantize_mx(out=h_cd[:, cols].bitcast(E4M3), scales=h_sc[:, cols], in_=h_bf[:, i, :])

        x_round(0, 0, 2, "V")
        wx_q.append(quantize(g_wx2, "wx2", E4M3))
        x_quantize(0, 0)
        x_round(1, 0, 2, "S")
        x_round(2, 0, 1, "V")
        x_quantize(1, 0)
        x_quantize(2, 0)
        x_round(2, 1, 2, "S")
        x_quantize(2, 1)
        x_round(3, 2, 4, "V")
        x_quantize(0, 2)
        x_round(4, 2, 3, "V")
        x_round(4, 3, 4, "S")
        h_product(0)
        x_quantize(1, 2)
        x_quantize(1, 3)
        x_round(5, 2, 3, "S")
        x_round(6, 3, 4, "V")
        x_quantize(2, 2)
        x_quantize(2, 3)
        h_product(1)
        h_product(2)
        h_product(3)
        for i in range(PACK):
            h_quantize(i)

        o_cd = keep.tile([P, M], U32, name="o_cd", align_bytes=64)
        o_sc = keep.tile([P, M], U8, name="o_sc", align_bytes=64)
        out_rows = out_0.rearrange("(p i) n -> p i n", i=PACK)
        out_words = out_1[0].rearrange("p n t -> p (n t)").bitcast(I32)
        units = []
        for ci, (n0, width) in enumerate(CHUNKS):
            per = BANK // width
            for i0 in range(0, PACK, per):
                units.append((ci, i0, per))
        o_tiles = [keep.tile([P, PACK, width], F32, name="o%d" % ci) for ci, (n0, width) in enumerate(CHUNKS)]
        y_banks, relus, views = {}, {}, {}

        def y_mul(u):
            ci, i0, per = units[u]
            n0, width = CHUNKS[ci]
            y_banks[u] = bank(u % 8)
            for s in range(per):
                cols = slice(P * (i0 + s), P * (i0 + s + 1))
                nc.tensor.matmul_mx(out=y_banks[u][:, width * s : width * (s + 1)], lhsT=h_cd[:, cols].bitcast(E4M3), lhsT_scale=h_sc[:, cols],
                                    rhs=w_cd[:, 2 * n0 : 2 * (n0 + width)].bitcast(E2M1), rhs_scale=w_sc[:, n0 : n0 + width],
                                    start=True, stop=True)

        def relu(u, engine):
            relus[u] = stage.tile([P, BANK], F32, name="relu", bufs=8)
            if engine == "S":
                nc.scalar.activation(out=relus[u][:], in_=y_banks[u][:], func=ACT.Relu)
            else:
                nc.vector.tensor_scalar_max(out=relus[u][:], in0=y_banks[u][:], scalar1=0.0)
            if u + 8 < len(units):
                y_mul(u + 8)

        def square(u):
            ci, i0, per = units[u]
            n0, width = CHUNKS[ci]
            nc.scalar.activation(out=o_tiles[ci][:, i0 : i0 + per, :].rearrange("p i n -> p (i n)"), in_=relus[u][:], func=ACT.Square)

        def rows_store(ci, i0, i1):
            n0, width = CHUNKS[ci]
            nc.sync.dma_start(out=out_rows[:, i0:i1, n0 : n0 + width], in_=o_tiles[ci][:, i0:i1, :])

        def o_round(ci):
            views[ci] = round_plain("V", o_tiles[ci][:])

        def o_quantize(ci):
            n0, width = CHUNKS[ci]
            nc.vector.quantize_mx(out=o_cd[:, n0 : n0 + width].bitcast(E4M3), scales=o_sc[:, n0 : n0 + width], in_=views[ci])

        def o_store(n0, n1):
            nc.sync.dma_start(out=out_words[:, n0:n1], in_=o_cd[:, n0:n1].bitcast(I32))

        def scale_store(queue, n0, n1):
            for q in range(4):
                queue.dma_start(out=out_2[0, 4 * q : 4 * q + 4, n0:n1].bitcast(I32), in_=o_sc[32 * q : 32 * q + 4, n0:n1].bitcast(I32))

        for u in range(8):
            y_mul(u)
        relu(0, "V")
        relu(1, "S")
        relu(2, "V")
        square(0)
        rows_store(0, 0, 1)
        relu(3, "V")
        square(1)
        rows_store(0, 1, 2)
        relu(4, "V")
        square(2)
        rows_store(0, 2, 3)
        relu(5, "V")
        square(3)
        rows_store(0, 3, 4)
        relu(6, "V")
        square(4)
        rows_store(1, 0, 1)
        relu(7, "V")
        square(5)
        rows_store(1, 1, 2)
        o_round(0)
        square(6)
        rows_store(1, 2, 3)
        square(7)
        rows_store(1, 3, 4)
        relu(8, "V")
        relu(9, "S")
        o_quantize(0)
        square(8)
        rows_store(2, 0, 2)
        o_store(0, 512)
        o_round(1)
        relu(10, "S")
        square(9)
        rows_store(2, 2, 4)
        relu(11, "S")
        o_quantize(1)
        square(10)
        rows_store(3, 0, 2)
        square(11)
        rows_store(3, 2, 4)
        o_store(512, 1024)
        o_round(2)
        o_quantize(2)
        o_round(3)
        o_store(1024, 1280)
        o_quantize(3)
        o_store(1280, 1536)
        scale_store(nc.scalar, 0, 1536)
